import numpy as np
import ml_dtypes


def mxq(x, axis, fmt="e4m3"):
    dtype, down = {"e4m3": (ml_dtypes.float8_e4m3fn, 7), "e5m2": (ml_dtypes.float8_e5m2, 14)}[fmt]
    v = np.moveaxis(np.asarray(x, np.float32).astype(ml_dtypes.bfloat16).astype(np.float64), axis, -1)
    blocks = v.reshape(v.shape[:-1] + (-1, 32))
    amax = np.abs(blocks).max(-1, keepdims=True)
    byte = np.maximum(np.where(amax > 0, np.frexp(amax)[1] - 1 + 127, 0) - down, 1)
    scale = np.exp2(byte - 127.0)
    codes = (blocks / scale).astype(np.float32).astype(dtype).astype(np.float64)
    return np.moveaxis((codes * scale).reshape(v.shape), -1, axis)


WIDE = False


def mx_kscale(k):
    if not WIDE:
        return np.ones(k)
    levels = np.array([10, -10, 5, -5, 0])
    if k % 512:
        return np.exp2(np.random.permutation(np.resize(levels, k // 32))).repeat(32)
    a = np.empty((k // 512, 16))
    for p in range(k // 512):
        a[p, :8] = np.random.permutation(np.resize(levels, 8))
        for g in range(8):
            far = levels[np.abs(levels - a[p, g]) >= 10]
            a[p, g + 8] = far[np.random.randint(len(far))]
    return np.exp2(a.ravel()).repeat(32)


def f64(x):
    return np.asarray(x).astype(np.float64)


def striped8(idx):
    return np.concatenate([v.reshape(-1, 16).T for v in idx]).astype(np.uint16)


def unstriped8(offs):
    return np.stack([offs[16 * g:16 * g + 16].T.reshape(-1) for g in range(8)]).astype(np.int64)


E2M1 = np.array([0.0, 0.5, 1.0, 1.5, 2.0, 3.0, 4.0, 6.0, -0.0, -0.5, -1.0, -1.5, -2.0, -3.0, -4.0, -6.0])


def pack_weight(w, fmt):
    k, n = w.shape
    w = f64(np.asarray(w, np.float32).astype(ml_dtypes.bfloat16)).reshape(k // 32, 32, n)
    amax = np.abs(w).max(1)
    if fmt == "e4m3":
        byte = np.frexp(amax)[1] - 1 + 127 - 7
    else:
        mant, ex = np.frexp(amax / 6.0)
        byte = np.where(mant > 0.5, ex, ex - 1) + 127
    byte = np.clip(np.where(amax > 0, byte, 1), 1, 254)
    scaled = (w * np.exp2(127.0 - byte)[:, None, :]).reshape(k, n).astype(np.float32)
    by_word = np.ascontiguousarray(scaled.reshape(k // 512, 128, 4, n).transpose(0, 1, 3, 2))
    if fmt == "e4m3":
        words = by_word.astype(ml_dtypes.float8_e4m3fn).view(np.uint8)
    else:
        c = by_word.astype(ml_dtypes.float4_e2m1fn).view(np.uint8) & 0xF
        words = (c[..., 0::2] | (c[..., 1::2] << 4)).reshape(k // 512, 128, 2 * n)
    return np.ascontiguousarray(words), np.ascontiguousarray(byte.astype(np.uint8).reshape(k // 512, 16, n))


def unpack_weight(words, scales, fmt):
    g, _, n = scales.shape
    words = np.ascontiguousarray(words).reshape(g, 128, n, -1)
    if fmt == "e4m3":
        vals = words.view(ml_dtypes.float8_e4m3fn).astype(np.float64)
    else:
        nib = np.empty((g, 128, n, 4), np.uint8)
        nib[..., 0::2] = words & 0xF
        nib[..., 1::2] = words >> 4
        vals = E2M1[nib]
    vals = vals * np.repeat(np.exp2(scales.astype(np.float64) - 127.0), 8, axis=1)[..., None]
    return vals.transpose(0, 1, 3, 2).reshape(g * 512, n)


K, M, T, S = 2048, 512, 1024, 512


def setup_inputs():
    n = np.random.standard_normal
    s = mx_kscale(K)[:, None]
    p_w = pack_weight(n((K, M)) / np.sqrt(K) / s, "e2m1")
    return {
        "xT": (n((K, T)) * s).astype(np.float32),
        "w_words": p_w[0],
        "w_scales": p_w[1],
        "wgt": np.repeat(np.random.uniform(0.5, 2.0, (8, S)), 16, axis=0).astype(np.float32),
        "r": (n((512, 512))).astype(np.float32),
        "offs": striped8(np.stack([np.random.permutation(T)[:S] for _ in range(8)])),
    }


def reference(xT, w_words, w_scales, wgt, r, offs):
    idx = unstriped8(offs)
    group = np.arange(K) % 512 // 64
    xg = f64(wgt)[np.arange(K) // 4 % 128] * f64(xT)[np.arange(K)[:, None], idx[group]]
    xT_ = mxq(xg, 0, "e4m3")
    w_ = unpack_weight(w_words, w_scales, "e2m1")
    y = xT_.T @ w_
    return f64(r) + y

@@ -1,0 +1,161 @@
+from contextlib import ExitStack
+
+import concourse.mybir as mybir
+
+K, M, T, S = 2048, 512, 1024, 512
+FLOPS = 2 * K * M * S
+
+F32 = mybir.dt.float32
+BF16 = mybir.dt.bfloat16
+I32 = mybir.dt.int32
+U32 = mybir.dt.uint32
+U16 = mybir.dt.uint16
+U8 = mybir.dt.uint8
+E4M3X4 = mybir.dt.float8_e4m3fn_x4
+E2M1X4 = mybir.dt.float4_e2m1fn_x4
+MULT = mybir.AluOpType.mult
+ADD = mybir.AluOpType.add
+
+P = 128
+PACK = 4
+K_PASS = P * PACK
+PASSES = K // K_PASS
+TOK = 128
+TOK_TILES = S // TOK
+PER_COL = 16
+
+
+def tile_list_heads_tm_res_kernel(tc, xT, w_words, w_scales, wgt, r, offs, out):
+    nc = tc.nc
+    with ExitStack() as ctx:
+        lists = ctx.enter_context(tc.tile_pool(name="lists", bufs=1))
+        keep = ctx.enter_context(tc.tile_pool(name="keep", bufs=1))
+        psum = ctx.enter_context(tc.psum_pool(name="psum", bufs=1))
+
+        offsets = lists.tile([P, S // PER_COL], U16, name="offsets")
+        x = [
+            [
+                keep.tile([P, T], F32, name=f"x{a}_{i}", tag="early" if (a, i) == (0, 2) else f"x{a}_{i}", align_bytes=64)
+                for i in range(PACK)
+            ]
+            for a in range(PASSES)
+        ]
+        wg = [keep.tile([P, 256], F32, name=f"wg{h}") for h in range(2)]
+        picked = [keep.tile([P, PACK, S], F32, name=f"picked{a}", align_bytes=64) for a in range(PASSES)]
+        grouped = [keep.tile([P, S, PACK], BF16, name=f"grouped{a}", align_bytes=64) for a in range(PASSES)]
+        codes = [keep.tile([P, S], U32, name=f"codes{a}", align_bytes=64) for a in range(PASSES)]
+        scales = [keep.tile([P, S], U8, name=f"scales{a}", align_bytes=64) for a in range(PASSES)]
+        ww = keep.tile([P, PASSES, 2 * M], U8, name="ww", align_bytes=64)
+        res = [keep.tile([P, M], F32, name=f"res{t}") for t in range(TOK_TILES)]
+        done = [keep.tile([P, M], F32, name=f"done{t}") for t in range(TOK_TILES)]
+        acc = [psum.tile([P, M], F32, name=f"acc{t}") for t in range(TOK_TILES)]
+
+        def load_x(a, i):
+            rows = xT[a * K_PASS : (a + 1) * K_PASS, :].rearrange("(p i) t -> p i t", i=PACK)
+            nc.sync.dma_start(out=x[a][i][:], in_=rows[:, i, :])
+
+        def gather(a, i, lo, hi):
+            half = lo // 256
+            nc.vector.tensor_tensor(
+                picked[a][:, i, lo:hi],
+                x[a][i][:].indirect(offsets[:, lo // PER_COL : hi // PER_COL]),
+                wg[half][:, lo - 256 * half : hi - 256 * half],
+                MULT,
+            )
+
+        def interleave(a, lo, hi):
+            nc.scalar.copy(
+                out=grouped[a][:, lo:hi, :].rearrange("p (c l) i -> p c i l", l=4),
+                in_=picked[a][:, :, lo:hi].rearrange("p i (c l) -> p c i l", l=4),
+            )
+
+        def quantise(a, lo, hi):
+            nc.vector.quantize_mx(
+                out=codes[a][:, lo:hi].bitcast(E4M3X4),
+                scales=scales[a][:, lo:hi],
+                in_=grouped[a][:, lo:hi, :].rearrange("p j i -> p (j i)"),
+            )
+
+        def multiply(ws, a, t):
+            cols = slice(t * TOK, (t + 1) * TOK)
+            nc.tensor.matmul_mx(
+                out=acc[t][:],
+                lhsT=codes[a][:, cols].bitcast(E4M3X4),
+                lhsT_scale=scales[a][:, cols],
+                rhs=ww[:, a, :].bitcast(E2M1X4),
+                rhs_scale=ws[:, a, :],
+                start=(a == 0),
+                stop=(a == PASSES - 1),
+            )
+
+        def finish(t):
+            rows = slice(t * TOK, (t + 1) * TOK)
+            nc.vector.tensor_tensor(done[t][:], acc[t][:], res[t][:], ADD)
+            nc.sync.dma_start(out=out[rows, :], in_=done[t][:])
+
+        nc.sync.dma_start(offsets[:], offs)
+        nc.scalar.dma_start(out=wg[0][:], in_=wgt[:, 0:256])
+        load_x(0, 0)
+        nc.sync.dma_start(out=wg[1][:], in_=wgt[:, 256:512])
+        for i in range(1, PACK):
+            load_x(0, i)
+        for i in range(PACK):
+            load_x(1, i)
+        nc.sync.dma_start(
+            out=ww[:].rearrange("p a n -> p (a n)").bitcast(I32).rearrange("p (a n) -> p a n", a=PASSES),
+            in_=w_words.rearrange("a p n -> p a n").bitcast(I32),
+        )
+        for a in range(2, PASSES):
+            for i in range(PACK):
+                load_x(a, i)
+        for t in range(TOK_TILES):
+            nc.sync.dma_start(out=res[t][:], in_=r[t * TOK : (t + 1) * TOK, :])
+
+        last = PASSES - 1
+        ws = None
+        for a in range(last):
+            for i in range(PACK):
+                gather(a, i, 0, 256)
+                gather(a, i, 256, 512)
+                if (a, i) == (0, 3):
+                    ws = keep.tile([P, PASSES, M], U8, name="ws", tag="early", align_bytes=64)
+                    nc.gpsimd.memset(ws[:].rearrange("p a n -> p (a n)").bitcast(I32), 0)
+                    for q in range(4):
+                        nc.scalar.dma_start(
+                            out=ws[32 * q : 32 * q + 4, :, :].bitcast(I32),
+                            in_=w_scales[:, 4 * q : 4 * q + 4, :].rearrange("a q n -> q a n").bitcast(I32),
+                        )
+                if i == 2 and a > 0:
+                    quantise(a - 1, 0, S)
+                    for t in range(TOK_TILES):
+                        multiply(ws, a - 1, t)
+            interleave(a, 0, 256)
+            interleave(a, 256, 512)
+
+        for i in range(PACK - 1):
+            gather(last, i, 0, 256)
+            gather(last, i, 256, 512)
+            if i == 2:
+                quantise(last - 1, 0, S)
+                for t in range(TOK_TILES):
+                    multiply(ws, last - 1, t)
+        gather(last, 3, 0, 256)
+        interleave(last, 0, 256)
+        gather(last, 3, 384, 512)
+        gather(last, 3, 256, 384)
+        nc.vector.tensor_copy(
+            out=grouped[last][:, 384:512, :].rearrange("p (c l) i -> p c i l", l=4),
+            in_=picked[last][:, :, 384:512].rearrange("p i (c l) -> p c i l", l=4),
+        )
+        interleave(last, 256, 384)
+        quantise(last, 0, 256)
+        multiply(ws, last, 0)
+        multiply(ws, last, 1)
+        quantise(last, 384, 512)
+        multiply(ws, last, 3)
+        quantise(last, 256, 384)
+        multiply(ws, last, 2)
+        finish(0)
+        finish(1)
+        finish(3)
+        finish(2)

@@ -35,12 +35,12 @@ def tile_list_heads_tm_res_kernel(tc, xT, w_words, w_scales, wgt, r, offs, out):
         offsets = lists.tile([P, S // PER_COL], U16, name="offsets")
         x = [
             [
-                keep.tile([P, T], F32, name=f"x{a}_{i}", tag="early" if (a, i) == (0, 2) else f"x{a}_{i}", align_bytes=64)
+                keep.tile([P, T], F32, name=f"x{a}_{i}", align_bytes=64)
                 for i in range(PACK)
             ]
             for a in range(PASSES)
         ]
-        wg = [keep.tile([P, 256], F32, name=f"wg{h}") for h in range(2)]
+        wg = keep.tile([P, S], F32, name="wg")
         picked = [keep.tile([P, PACK, S], F32, name=f"picked{a}", align_bytes=64) for a in range(PASSES)]
         grouped = [keep.tile([P, S, PACK], BF16, name=f"grouped{a}", align_bytes=64) for a in range(PASSES)]
         codes = [keep.tile([P, S], U32, name=f"codes{a}", align_bytes=64) for a in range(PASSES)]
@@ -55,11 +55,10 @@ def tile_list_heads_tm_res_kernel(tc, xT, w_words, w_scales, wgt, r, offs, out):
             nc.sync.dma_start(out=x[a][i][:], in_=rows[:, i, :])
 
         def gather(a, i, lo, hi):
-            half = lo // 256
             nc.vector.tensor_tensor(
                 picked[a][:, i, lo:hi],
                 x[a][i][:].indirect(offsets[:, lo // PER_COL : hi // PER_COL]),
-                wg[half][:, lo - 256 * half : hi - 256 * half],
+                wg[:, lo:hi],
                 MULT,
             )
 
@@ -93,38 +92,37 @@ def tile_list_heads_tm_res_kernel(tc, xT, w_words, w_scales, wgt, r, offs, out):
             nc.vector.tensor_tensor(done[t][:], acc[t][:], res[t][:], ADD)
             nc.sync.dma_start(out=out[rows, :], in_=done[t][:])
 
+        ws = keep.tile([P, PASSES, M], U8, name="ws", align_bytes=64)
+        nc.gpsimd.memset(ws[:].rearrange("p a n -> p (a n)").bitcast(I32), 0)
         nc.sync.dma_start(offsets[:], offs)
-        nc.scalar.dma_start(out=wg[0][:], in_=wgt[:, 0:256])
+        nc.scalar.dma_start(out=wg[:, 0:256], in_=wgt[:, 0:256])
         load_x(0, 0)
-        nc.sync.dma_start(out=wg[1][:], in_=wgt[:, 256:512])
-        for i in range(1, PACK):
-            load_x(0, i)
-        for i in range(PACK):
-            load_x(1, i)
-        nc.sync.dma_start(
-            out=ww[:].rearrange("p a n -> p (a n)").bitcast(I32).rearrange("p (a n) -> p a n", a=PASSES),
-            in_=w_words.rearrange("a p n -> p a n").bitcast(I32),
-        )
-        for a in range(2, PASSES):
+        nc.sync.dma_start(out=wg[:, 256:512], in_=wgt[:, 256:512])
+        for a in range(PASSES):
             for i in range(PACK):
-                load_x(a, i)
+                if (a, i) == (PASSES - 1, 2):
+                    for q in range(4):
+                        nc.sync.dma_start(
+                            out=ws[32 * q : 32 * q + 4, :, :].bitcast(I32),
+                            in_=w_scales[:, 4 * q : 4 * q + 4, :].rearrange("a q n -> q a n").bitcast(I32),
+                        )
+                    nc.sync.dma_start(
+                        out=ww[:].rearrange("p a n -> p (a n)").bitcast(I32).rearrange("p (a n) -> p a n", a=PASSES),
+                        in_=w_words.rearrange("a p n -> p a n").bitcast(I32),
+                    )
+                if (a, i) != (0, 0):
+                    load_x(a, i)
         for t in range(TOK_TILES):
             nc.sync.dma_start(out=res[t][:], in_=r[t * TOK : (t + 1) * TOK, :])
 
         last = PASSES - 1
-        ws = None
         for a in range(last):
             for i in range(PACK):
-                gather(a, i, 0, 256)
-                gather(a, i, 256, 512)
-                if (a, i) == (0, 3):
-                    ws = keep.tile([P, PASSES, M], U8, name="ws", tag="early", align_bytes=64)
-                    nc.gpsimd.memset(ws[:].rearrange("p a n -> p (a n)").bitcast(I32), 0)
-                    for q in range(4):
-                        nc.scalar.dma_start(
-                            out=ws[32 * q : 32 * q + 4, :, :].bitcast(I32),
-                            in_=w_scales[:, 4 * q : 4 * q + 4, :].rearrange("a q n -> q a n").bitcast(I32),
-                        )
+                if (a, i) == (0, 0) or i == PACK - 1:
+                    gather(a, i, 0, 256)
+                    gather(a, i, 256, 512)
+                else:
+                    gather(a, i, 0, S)
                 if i == 2 and a > 0:
                     quantise(a - 1, 0, S)
                     for t in range(TOK_TILES):
@@ -133,8 +131,7 @@ def tile_list_heads_tm_res_kernel(tc, xT, w_words, w_scales, wgt, r, offs, out):
             interleave(a, 256, 512)
 
         for i in range(PACK - 1):
-            gather(last, i, 0, 256)
-            gather(last, i, 256, 512)
+            gather(last, i, 0, S)
             if i == 2:
                 quantise(last - 1, 0, S)
                 for t in range(TOK_TILES):

@@ -68,6 +68,12 @@ def tile_list_heads_tm_res_kernel(tc, xT, w_words, w_scales, wgt, r, offs, out):
                 in_=picked[a][:, :, lo:hi].rearrange("p i (c l) -> p c i l", l=4),
             )
 
+        def interleave_pair(a, i, lo, hi):
+            nc.scalar.copy(
+                out=grouped[a][:, lo:hi, i : i + 2].rearrange("p (c l) i -> p c i l", l=4),
+                in_=picked[a][:, i : i + 2, lo:hi].rearrange("p i (c l) -> p c i l", l=4),
+            )
+
         def quantise(a, lo, hi):
             nc.vector.quantize_mx(
                 out=codes[a][:, lo:hi].bitcast(E4M3X4),
@@ -132,27 +138,17 @@ def tile_list_heads_tm_res_kernel(tc, xT, w_words, w_scales, wgt, r, offs, out):
 
         for i in range(PACK - 1):
             gather(last, i, 0, S)
+            if i == 1:
+                interleave_pair(last, 0, 0, S)
             if i == 2:
                 quantise(last - 1, 0, S)
                 for t in range(TOK_TILES):
                     multiply(ws, last - 1, t)
-        gather(last, 3, 0, 256)
-        interleave(last, 0, 256)
-        gather(last, 3, 384, 512)
-        gather(last, 3, 256, 384)
-        nc.vector.tensor_copy(
-            out=grouped[last][:, 384:512, :].rearrange("p (c l) i -> p c i l", l=4),
-            in_=picked[last][:, :, 384:512].rearrange("p i (c l) -> p c i l", l=4),
-        )
-        interleave(last, 256, 384)
-        quantise(last, 0, 256)
-        multiply(ws, last, 0)
-        multiply(ws, last, 1)
-        quantise(last, 384, 512)
-        multiply(ws, last, 3)
-        quantise(last, 256, 384)
-        multiply(ws, last, 2)
-        finish(0)
-        finish(1)
-        finish(3)
-        finish(2)
+        for t in range(TOK_TILES):
+            gather(last, 3, t * TOK, (t + 1) * TOK)
+            interleave_pair(last, 2, t * TOK, (t + 1) * TOK)
+        for t in range(TOK_TILES):
+            quantise(last, t * TOK, (t + 1) * TOK)
+            multiply(ws, last, t)
+        for t in range(TOK_TILES):
+            finish(t)

@@ -22,6 +22,7 @@ K_PASS = P * PACK
 PASSES = K // K_PASS
 TOK = 128
 TOK_TILES = S // TOK
+HALF = S // 2
 PER_COL = 16
 
 
@@ -32,21 +33,22 @@ def tile_list_heads_tm_res_kernel(tc, xT, w_words, w_scales, wgt, r, offs, out):
         keep = ctx.enter_context(tc.tile_pool(name="keep", bufs=1))
         psum = ctx.enter_context(tc.psum_pool(name="psum", bufs=1))
 
+        last = PASSES - 1
         offsets = lists.tile([P, S // PER_COL], U16, name="offsets")
-        x = [
-            [
-                keep.tile([P, T], F32, name=f"x{a}_{i}", align_bytes=64)
-                for i in range(PACK)
-            ]
-            for a in range(PASSES)
-        ]
+        x = [[keep.tile([P, T], F32, name=f"x{a}_{i}", align_bytes=64) for i in range(PACK)] for a in range(PASSES)]
         wg = keep.tile([P, S], F32, name="wg")
-        picked = [keep.tile([P, PACK, S], F32, name=f"picked{a}", align_bytes=64) for a in range(PASSES)]
+        picked = [keep.tile([P, PACK, S], F32, name=f"picked{a}", align_bytes=64) for a in range(last)]
+        low = keep.tile([P, 2, S], F32, name="low", align_bytes=64)
+        high = keep.tile([P, 3, HALF], F32, name="high", align_bytes=64)
+        high_a = high[:, 0:2, :]
+        high_b = high[:, 0:3:2, :]
         grouped = [keep.tile([P, S, PACK], BF16, name=f"grouped{a}", align_bytes=64) for a in range(PASSES)]
         codes = [keep.tile([P, S], U32, name=f"codes{a}", align_bytes=64) for a in range(PASSES)]
         scales = [keep.tile([P, S], U8, name=f"scales{a}", align_bytes=64) for a in range(PASSES)]
-        ww = keep.tile([P, PASSES, 2 * M], U8, name="ww", align_bytes=64)
-        res = [keep.tile([P, M], F32, name=f"res{t}") for t in range(TOK_TILES)]
+        word_loads = ((0, 3), (3, 1))
+        ww = [keep.tile([P, n, 2 * M], U8, name=f"ww{a}", align_bytes=64) for a, n in word_loads]
+        ws = keep.tile([P, PASSES, M], U8, name="ws", align_bytes=64)
+        res = [keep.tile([P, n, M], F32, name=f"res{t}") for t, n in ((0, 1), (1, 3))]
         done = [keep.tile([P, M], F32, name=f"done{t}") for t in range(TOK_TILES)]
         acc = [psum.tile([P, M], F32, name=f"acc{t}") for t in range(TOK_TILES)]
 
@@ -54,24 +56,41 @@ def tile_list_heads_tm_res_kernel(tc, xT, w_words, w_scales, wgt, r, offs, out):
             rows = xT[a * K_PASS : (a + 1) * K_PASS, :].rearrange("(p i) t -> p i t", i=PACK)
             nc.sync.dma_start(out=x[a][i][:], in_=rows[:, i, :])
 
+        def load_scales():
+            for q in range(4):
+                nc.sync.dma_start(
+                    out=ws[32 * q : 32 * q + 4, :, :].bitcast(I32),
+                    in_=w_scales[:, 4 * q : 4 * q + 4, :].rearrange("a q n -> q a n").bitcast(I32),
+                )
+
+        def load_words(h):
+            first, n = word_loads[h]
+            nc.sync.dma_start(
+                out=ww[h][:].bitcast(I32),
+                in_=w_words[first : first + n].rearrange("a p n -> p a n").bitcast(I32),
+            )
+
+        def rows_of(a, i, n, lo, hi):
+            if a < last:
+                return picked[a][:, i : i + n, lo:hi]
+            if i < 2:
+                return low[:, i : i + n, lo:hi]
+            if lo < HALF:
+                return high_a[:, i - 2 : i - 2 + n, lo:hi]
+            return high_b[:, i - 2 : i - 2 + n, lo - HALF : hi - HALF]
+
         def gather(a, i, lo, hi):
             nc.vector.tensor_tensor(
-                picked[a][:, i, lo:hi],
+                rows_of(a, i, 1, lo, hi).rearrange("p i j -> p (i j)"),
                 x[a][i][:].indirect(offsets[:, lo // PER_COL : hi // PER_COL]),
                 wg[:, lo:hi],
                 MULT,
             )
 
-        def interleave(a, lo, hi):
+        def interleave(a, i, n, lo, hi):
             nc.scalar.copy(
-                out=grouped[a][:, lo:hi, :].rearrange("p (c l) i -> p c i l", l=4),
-                in_=picked[a][:, :, lo:hi].rearrange("p i (c l) -> p c i l", l=4),
-            )
-
-        def interleave_pair(a, i, lo, hi):
-            nc.scalar.copy(
-                out=grouped[a][:, lo:hi, i : i + 2].rearrange("p (c l) i -> p c i l", l=4),
-                in_=picked[a][:, i : i + 2, lo:hi].rearrange("p i (c l) -> p c i l", l=4),
+                out=grouped[a][:, lo:hi, i : i + n].rearrange("p (c l) i -> p c i l", l=4),
+                in_=rows_of(a, i, n, lo, hi).rearrange("p i (c l) -> p c i l", l=4),
             )
 
         def quantise(a, lo, hi):
@@ -81,74 +100,72 @@ def tile_list_heads_tm_res_kernel(tc, xT, w_words, w_scales, wgt, r, offs, out):
                 in_=grouped[a][:, lo:hi, :].rearrange("p j i -> p (j i)"),
             )
 
-        def multiply(ws, a, t):
+        def multiply(a, t):
             cols = slice(t * TOK, (t + 1) * TOK)
             nc.tensor.matmul_mx(
                 out=acc[t][:],
                 lhsT=codes[a][:, cols].bitcast(E4M3X4),
                 lhsT_scale=scales[a][:, cols],
-                rhs=ww[:, a, :].bitcast(E2M1X4),
+                rhs=ww[a // last][:, a % last, :].bitcast(E2M1X4),
                 rhs_scale=ws[:, a, :],
                 start=(a == 0),
-                stop=(a == PASSES - 1),
+                stop=(a == last),
             )
 
-        def finish(t):
-            rows = slice(t * TOK, (t + 1) * TOK)
-            nc.vector.tensor_tensor(done[t][:], acc[t][:], res[t][:], ADD)
-            nc.sync.dma_start(out=out[rows, :], in_=done[t][:])
+        def finish(t, lo, hi):
+            residual = res[min(t, 1)][:, max(t - 1, 0), lo:hi]
+            nc.vector.tensor_tensor(done[t][:, lo:hi], acc[t][:, lo:hi], residual, ADD)
+            nc.sync.dma_start(out=out[t * TOK : (t + 1) * TOK, lo:hi], in_=done[t][:, lo:hi])
 
-        ws = keep.tile([P, PASSES, M], U8, name="ws", align_bytes=64)
         nc.gpsimd.memset(ws[:].rearrange("p a n -> p (a n)").bitcast(I32), 0)
         nc.sync.dma_start(offsets[:], offs)
-        nc.scalar.dma_start(out=wg[:, 0:256], in_=wgt[:, 0:256])
+        nc.scalar.dma_start(out=wg[:, 0:HALF], in_=wgt[:, 0:HALF])
         load_x(0, 0)
-        nc.sync.dma_start(out=wg[:, 256:512], in_=wgt[:, 256:512])
+        nc.sync.dma_start(out=wg[:, HALF:S], in_=wgt[:, HALF:S])
         for a in range(PASSES):
             for i in range(PACK):
-                if (a, i) == (PASSES - 1, 2):
-                    for q in range(4):
-                        nc.sync.dma_start(
-                            out=ws[32 * q : 32 * q + 4, :, :].bitcast(I32),
-                            in_=w_scales[:, 4 * q : 4 * q + 4, :].rearrange("a q n -> q a n").bitcast(I32),
-                        )
-                    nc.sync.dma_start(
-                        out=ww[:].rearrange("p a n -> p (a n)").bitcast(I32).rearrange("p (a n) -> p a n", a=PASSES),
-                        in_=w_words.rearrange("a p n -> p a n").bitcast(I32),
-                    )
+                if (a, i) == (last, 2):
+                    load_scales()
+                    load_words(0)
                 if (a, i) != (0, 0):
                     load_x(a, i)
-        for t in range(TOK_TILES):
-            nc.sync.dma_start(out=res[t][:], in_=r[t * TOK : (t + 1) * TOK, :])
+        load_words(1)
+        nc.sync.dma_start(out=res[0][:, 0, :], in_=r[0:TOK, :])
+        nc.sync.dma_start(out=res[1][:], in_=r[TOK:S, :].rearrange("(t p) n -> p t n", p=P))
 
-        last = PASSES - 1
         for a in range(last):
             for i in range(PACK):
                 if (a, i) == (0, 0) or i == PACK - 1:
-                    gather(a, i, 0, 256)
-                    gather(a, i, 256, 512)
+                    gather(a, i, 0, HALF)
+                    gather(a, i, HALF, S)
                 else:
                     gather(a, i, 0, S)
                 if i == 2 and a > 0:
                     quantise(a - 1, 0, S)
                     for t in range(TOK_TILES):
-                        multiply(ws, a - 1, t)
-            interleave(a, 0, 256)
-            interleave(a, 256, 512)
+                        multiply(a - 1, t)
+            interleave(a, 0, PACK, 0, HALF)
+            interleave(a, 0, PACK, HALF, S)
 
-        for i in range(PACK - 1):
-            gather(last, i, 0, S)
-            if i == 1:
-                interleave_pair(last, 0, 0, S)
-            if i == 2:
-                quantise(last - 1, 0, S)
-                for t in range(TOK_TILES):
-                    multiply(ws, last - 1, t)
+        gather(last, 0, 0, S)
+        gather(last, 1, 0, S)
+        interleave(last, 0, 2, 0, S)
+        quantise(last - 1, 0, S)
         for t in range(TOK_TILES):
+            multiply(last - 1, t)
+        gather(last, 2, 0, HALF)
+        for t in (0, 1):
             gather(last, 3, t * TOK, (t + 1) * TOK)
-            interleave_pair(last, 2, t * TOK, (t + 1) * TOK)
-        for t in range(TOK_TILES):
+            interleave(last, 2, 2, t * TOK, (t + 1) * TOK)
+        gather(last, 3, HALF, S)
+        quantise(last, 0, TOK)
+        multiply(last, 0)
+        for t in (2, 3):
+            gather(last, 2, t * TOK, (t + 1) * TOK)
+            interleave(last, 2, 2, t * TOK, (t + 1) * TOK)
+        for t in range(1, TOK_TILES):
             quantise(last, t * TOK, (t + 1) * TOK)
-            multiply(ws, last, t)
-        for t in range(TOK_TILES):
-            finish(t)
+            multiply(last, t)
+            finish(t - 1, 0, M)
+        finish(TOK_TILES - 1, 0, M // 2)
+        finish(TOK_TILES - 1, M // 2, M)

@@ -57,10 +57,10 @@ def tile_list_heads_tm_res_kernel(tc, xT, w_words, w_scales, wgt, r, offs, out):
             nc.sync.dma_start(out=x[a][i][:], in_=rows[:, i, :])
 
         def load_scales():
-            for q in range(4):
+            for u in range(4):
                 nc.sync.dma_start(
-                    out=ws[32 * q : 32 * q + 4, :, :].bitcast(I32),
-                    in_=w_scales[:, 4 * q : 4 * q + 4, :].rearrange("a q n -> q a n").bitcast(I32),
+                    out=ws[u:P:32, :, :].bitcast(I32),
+                    in_=w_scales[:, u:16:4, :].rearrange("a q n -> q a n").bitcast(I32),
                 )
 
         def load_words(h):

@@ -23,6 +23,7 @@ PASSES = K // K_PASS
 TOK = 128
 TOK_TILES = S // TOK
 HALF = S // 2
+CUT = 192
 PER_COL = 16
 
 
@@ -42,13 +43,13 @@ def tile_list_heads_tm_res_kernel(tc, xT, w_words, w_scales, wgt, r, offs, out):
         high = keep.tile([P, 3, HALF], F32, name="high", align_bytes=64)
         high_a = high[:, 0:2, :]
         high_b = high[:, 0:3:2, :]
-        grouped = [keep.tile([P, S, PACK], BF16, name=f"grouped{a}", align_bytes=64) for a in range(PASSES)]
-        codes = [keep.tile([P, S], U32, name=f"codes{a}", align_bytes=64) for a in range(PASSES)]
-        scales = [keep.tile([P, S], U8, name=f"scales{a}", align_bytes=64) for a in range(PASSES)]
+        grouped = keep.tile([P, PASSES * S, PACK], BF16, name="grouped", align_bytes=64)
+        codes = keep.tile([P, PASSES * S], U32, name="codes", align_bytes=64)
+        scales = keep.tile([P, PASSES * S], U8, name="scales", align_bytes=64)
         word_loads = ((0, 3), (3, 1))
         ww = [keep.tile([P, n, 2 * M], U8, name=f"ww{a}", align_bytes=64) for a, n in word_loads]
         ws = keep.tile([P, PASSES, M], U8, name="ws", align_bytes=64)
-        res = [keep.tile([P, n, M], F32, name=f"res{t}") for t, n in ((0, 1), (1, 3))]
+        res = [keep.tile([P, n, M], F32, name=f"res{t}") for t, n in ((0, 1), (1, 1), (2, 2))]
         done = [keep.tile([P, M], F32, name=f"done{t}") for t in range(TOK_TILES)]
         acc = [psum.tile([P, M], F32, name=f"acc{t}") for t in range(TOK_TILES)]
 
@@ -89,38 +90,41 @@ def tile_list_heads_tm_res_kernel(tc, xT, w_words, w_scales, wgt, r, offs, out):
 
         def interleave(a, i, n, lo, hi):
             nc.scalar.copy(
-                out=grouped[a][:, lo:hi, i : i + n].rearrange("p (c l) i -> p c i l", l=4),
+                out=grouped[:, a * S + lo : a * S + hi, i : i + n].rearrange("p (c l) i -> p c i l", l=4),
                 in_=rows_of(a, i, n, lo, hi).rearrange("p i (c l) -> p c i l", l=4),
             )
 
         def quantise(a, lo, hi):
+            cols = slice(a * S + lo, a * S + hi)
             nc.vector.quantize_mx(
-                out=codes[a][:, lo:hi].bitcast(E4M3X4),
-                scales=scales[a][:, lo:hi],
-                in_=grouped[a][:, lo:hi, :].rearrange("p j i -> p (j i)"),
+                out=codes[:, cols].bitcast(E4M3X4),
+                scales=scales[:, cols],
+                in_=grouped[:, cols, :].rearrange("p j i -> p (j i)"),
             )
 
         def multiply(a, t):
-            cols = slice(t * TOK, (t + 1) * TOK)
+            cols = slice(a * S + t * TOK, a * S + (t + 1) * TOK)
             nc.tensor.matmul_mx(
                 out=acc[t][:],
-                lhsT=codes[a][:, cols].bitcast(E4M3X4),
-                lhsT_scale=scales[a][:, cols],
+                lhsT=codes[:, cols].bitcast(E4M3X4),
+                lhsT_scale=scales[:, cols],
                 rhs=ww[a // last][:, a % last, :].bitcast(E2M1X4),
                 rhs_scale=ws[:, a, :],
                 start=(a == 0),
                 stop=(a == last),
             )
 
-        def finish(t, lo, hi):
-            residual = res[min(t, 1)][:, max(t - 1, 0), lo:hi]
+        def add_residual(t, lo, hi):
+            residual = res[min(t, 2)][:, max(t - 2, 0), lo:hi]
             nc.vector.tensor_tensor(done[t][:, lo:hi], acc[t][:, lo:hi], residual, ADD)
-            nc.sync.dma_start(out=out[t * TOK : (t + 1) * TOK, lo:hi], in_=done[t][:, lo:hi])
+
+        def store(t):
+            nc.sync.dma_start(out=out[t * TOK : (t + 1) * TOK, :], in_=done[t][:])
 
         nc.gpsimd.memset(ws[:].rearrange("p a n -> p (a n)").bitcast(I32), 0)
-        nc.sync.dma_start(offsets[:], offs)
-        nc.scalar.dma_start(out=wg[:, 0:HALF], in_=wgt[:, 0:HALF])
         load_x(0, 0)
+        nc.scalar.dma_start(out=wg[:, 0:HALF], in_=wgt[:, 0:HALF])
+        nc.sync.dma_start(offsets[:], offs)
         nc.sync.dma_start(out=wg[:, HALF:S], in_=wgt[:, HALF:S])
         for a in range(PASSES):
             for i in range(PACK):
@@ -131,21 +135,29 @@ def tile_list_heads_tm_res_kernel(tc, xT, w_words, w_scales, wgt, r, offs, out):
                     load_x(a, i)
         load_words(1)
         nc.sync.dma_start(out=res[0][:, 0, :], in_=r[0:TOK, :])
-        nc.sync.dma_start(out=res[1][:], in_=r[TOK:S, :].rearrange("(t p) n -> p t n", p=P))
+        nc.sync.dma_start(out=res[1][:, 0, :], in_=r[TOK : 2 * TOK, :])
+        nc.sync.dma_start(out=res[2][:], in_=r[2 * TOK : S, :].rearrange("(t p) n -> p t n", p=P))
 
         for a in range(last):
             for i in range(PACK):
-                if (a, i) == (0, 0) or i == PACK - 1:
+                if (a, i) == (0, 0):
                     gather(a, i, 0, HALF)
                     gather(a, i, HALF, S)
+                elif i == PACK - 1 and a > 0:
+                    gather(a, i, 0, CUT)
+                    gather(a, i, CUT, S)
                 else:
                     gather(a, i, 0, S)
-                if i == 2 and a > 0:
-                    quantise(a - 1, 0, S)
-                    for t in range(TOK_TILES):
-                        multiply(a - 1, t)
-            interleave(a, 0, PACK, 0, HALF)
-            interleave(a, 0, PACK, HALF, S)
+                if (a, i) == (2, 2):
+                    quantise(0, 0, 2 * S)
+                    for b in (0, 1):
+                        for t in range(TOK_TILES):
+                            multiply(b, t)
+            if a == 0:
+                interleave(a, 0, PACK, 0, S)
+            else:
+                interleave(a, 0, PACK, 0, CUT)
+                interleave(a, 0, PACK, CUT, S)
 
         gather(last, 0, 0, S)
         gather(last, 1, 0, S)
@@ -163,9 +175,17 @@ def tile_list_heads_tm_res_kernel(tc, xT, w_words, w_scales, wgt, r, offs, out):
         for t in (2, 3):
             gather(last, 2, t * TOK, (t + 1) * TOK)
             interleave(last, 2, 2, t * TOK, (t + 1) * TOK)
-        for t in range(1, TOK_TILES):
-            quantise(last, t * TOK, (t + 1) * TOK)
-            multiply(last, t)
-            finish(t - 1, 0, M)
-        finish(TOK_TILES - 1, 0, M // 2)
-        finish(TOK_TILES - 1, M // 2, M)
+        quantise(last, TOK, 2 * TOK)
+        multiply(last, 1)
+        add_residual(0, 0, M)
+        store(0)
+        quantise(last, 2 * TOK, 3 * TOK)
+        multiply(last, 2)
+        add_residual(1, 0, M // 2)
+        quantise(last, 3 * TOK, S)
+        multiply(last, 3)
+        add_residual(1, M // 2, M)
+        store(1)
+        for t in (2, 3):
+            add_residual(t, 0, M)
+            store(t)

@@ -38,11 +38,9 @@ def tile_list_heads_tm_res_kernel(tc, xT, w_words, w_scales, wgt, r, offs, out):
         offsets = lists.tile([P, S // PER_COL], U16, name="offsets")
         x = [[keep.tile([P, T], F32, name=f"x{a}_{i}", align_bytes=64) for i in range(PACK)] for a in range(PASSES)]
         wg = keep.tile([P, S], F32, name="wg")
-        picked = [keep.tile([P, PACK, S], F32, name=f"picked{a}", align_bytes=64) for a in range(last)]
-        low = keep.tile([P, 2, S], F32, name="low", align_bytes=64)
-        high = keep.tile([P, 3, HALF], F32, name="high", align_bytes=64)
-        high_a = high[:, 0:2, :]
-        high_b = high[:, 0:3:2, :]
+        picked = [keep.tile([P, PACK, S], F32, name=f"picked{a}", align_bytes=64) for a in range(PASSES)]
+        slots = picked[last][:].rearrange("p i (t j) -> p (i t) j", t=TOK_TILES)
+        late_slot = {2: 2 * TOK_TILES, 3: 3 * TOK_TILES}
         grouped = keep.tile([P, PASSES * S, PACK], BF16, name="grouped", align_bytes=64)
         codes = keep.tile([P, PASSES * S], U32, name="codes", align_bytes=64)
         scales = keep.tile([P, PASSES * S], U8, name="scales", align_bytes=64)
@@ -72,13 +70,12 @@ def tile_list_heads_tm_res_kernel(tc, xT, w_words, w_scales, wgt, r, offs, out):
             )
 
         def rows_of(a, i, n, lo, hi):
-            if a < last:
-                return picked[a][:, i : i + n, lo:hi]
-            if i < 2:
-                return low[:, i : i + n, lo:hi]
-            if lo < HALF:
-                return high_a[:, i - 2 : i - 2 + n, lo:hi]
-            return high_b[:, i - 2 : i - 2 + n, lo - HALF : hi - HALF]
+            if a == last and i == 2 and lo >= HALF:
+                t = lo // TOK
+                first = late_slot[t]
+                step = 3 * TOK_TILES + t - first
+                return slots[:, first : first + (n - 1) * step + 1 : step, :]
+            return picked[a][:, i : i + n, lo:hi]
 
         def gather(a, i, lo, hi):
             nc.vector.tensor_tensor(
@@ -161,14 +158,16 @@ def tile_list_heads_tm_res_kernel(tc, xT, w_words, w_scales, wgt, r, offs, out):
 
         gather(last, 0, 0, S)
         gather(last, 1, 0, S)
-        interleave(last, 0, 2, 0, S)
+        interleave(last, 0, 2, 0, TOK)
+        interleave(last, 0, 2, HALF, S)
         quantise(last - 1, 0, S)
         for t in range(TOK_TILES):
             multiply(last - 1, t)
         gather(last, 2, 0, HALF)
-        for t in (0, 1):
-            gather(last, 3, t * TOK, (t + 1) * TOK)
-            interleave(last, 2, 2, t * TOK, (t + 1) * TOK)
+        gather(last, 3, 0, TOK)
+        interleave(last, 2, 2, 0, TOK)
+        gather(last, 3, TOK, HALF)
+        interleave(last, 0, PACK, TOK, HALF)
         gather(last, 3, HALF, S)
         quantise(last, 0, TOK)
         multiply(last, 0)

@@ -23,7 +23,6 @@ PASSES = K // K_PASS
 TOK = 128
 TOK_TILES = S // TOK
 HALF = S // 2
-CUT = 192
 PER_COL = 16
 
 
@@ -38,10 +37,14 @@ def tile_list_heads_tm_res_kernel(tc, xT, w_words, w_scales, wgt, r, offs, out):
         offsets = lists.tile([P, S // PER_COL], U16, name="offsets")
         x = [[keep.tile([P, T], F32, name=f"x{a}_{i}", align_bytes=64) for i in range(PACK)] for a in range(PASSES)]
         wg = keep.tile([P, S], F32, name="wg")
-        picked = [keep.tile([P, PACK, S], F32, name=f"picked{a}", align_bytes=64) for a in range(PASSES)]
-        slots = picked[last][:].rearrange("p i (t j) -> p (i t) j", t=TOK_TILES)
-        late_slot = {2: 2 * TOK_TILES, 3: 3 * TOK_TILES}
-        grouped = keep.tile([P, PASSES * S, PACK], BF16, name="grouped", align_bytes=64)
+        picked = [keep.tile([P, PACK * S], F32, name=f"picked{a}", align_bytes=64)[:] for a in (0, 2, 3)]
+        units = [(0, 0), (0, 1), (0, 2), (1, 0), (1, 1), (1, 2), (1, 3), (0, 3)]
+        units = units + [(2, 0), (2, 1), (2, 2), (3, 0), (2, 3), (3, 1), (3, 2), (3, 3)]
+        early = 2 * TOK_TILES
+        unit_words = TOK * PACK // 2
+        shared = keep.tile([P, (early - 1) * unit_words + PACK * S], F32, name="shared", align_bytes=64)
+        picked.insert(1, shared[:, (early - 1) * unit_words :])
+        late = keep.tile([P, (len(units) - early) * TOK * PACK], BF16, name="late", align_bytes=64)
         codes = keep.tile([P, PASSES * S], U32, name="codes", align_bytes=64)
         scales = keep.tile([P, PASSES * S], U8, name="scales", align_bytes=64)
         word_loads = ((0, 3), (3, 1))
@@ -50,6 +53,11 @@ def tile_list_heads_tm_res_kernel(tc, xT, w_words, w_scales, wgt, r, offs, out):
         res = [keep.tile([P, n, M], F32, name=f"res{t}") for t, n in ((0, 1), (1, 1), (2, 2))]
         done = [keep.tile([P, M], F32, name=f"done{t}") for t in range(TOK_TILES)]
         acc = [psum.tile([P, M], F32, name=f"acc{t}") for t in range(TOK_TILES)]
+
+        def slot(a, i, t):
+            if (a, i, t) == (last, 3, 0):
+                return 2 * S + HALF + TOK // 2
+            return i * S + t * TOK
 
         def load_x(a, i):
             rows = xT[a * K_PASS : (a + 1) * K_PASS, :].rearrange("(p i) t -> p i t", i=PACK)
@@ -69,38 +77,39 @@ def tile_list_heads_tm_res_kernel(tc, xT, w_words, w_scales, wgt, r, offs, out):
                 in_=w_words[first : first + n].rearrange("a p n -> p a n").bitcast(I32),
             )
 
-        def rows_of(a, i, n, lo, hi):
-            if a == last and i == 2 and lo >= HALF:
-                t = lo // TOK
-                first = late_slot[t]
-                step = 3 * TOK_TILES + t - first
-                return slots[:, first : first + (n - 1) * step + 1 : step, :]
-            return picked[a][:, i : i + n, lo:hi]
-
-        def gather(a, i, lo, hi):
+        def gather(a, i, t, n):
+            at = slot(a, i, t)
             nc.vector.tensor_tensor(
-                rows_of(a, i, 1, lo, hi).rearrange("p i j -> p (i j)"),
-                x[a][i][:].indirect(offsets[:, lo // PER_COL : hi // PER_COL]),
-                wg[:, lo:hi],
+                picked[a][:, at : at + n * TOK],
+                x[a][i][:].indirect(offsets[:, t * TOK // PER_COL : (t + n) * TOK // PER_COL]),
+                wg[:, t * TOK : (t + n) * TOK],
                 MULT,
             )
 
-        def interleave(a, i, n, lo, hi):
-            nc.scalar.copy(
-                out=grouped[:, a * S + lo : a * S + hi, i : i + n].rearrange("p (c l) i -> p c i l", l=4),
-                in_=rows_of(a, i, n, lo, hi).rearrange("p i (c l) -> p c i l", l=4),
-            )
+        def words_of(u, n):
+            if u < early:
+                return shared[:, u * unit_words : (u + n) * unit_words].bitcast(BF16)
+            return late[:, (u - early) * TOK * PACK : (u - early + n) * TOK * PACK]
 
-        def quantise(a, lo, hi):
-            cols = slice(a * S + lo, a * S + hi)
-            nc.vector.quantize_mx(
-                out=codes[:, cols].bitcast(E4M3X4),
-                scales=scales[:, cols],
-                in_=grouped[:, cols, :].rearrange("p j i -> p (j i)"),
-            )
+        def interleave(a, i, rows, t, n):
+            first = slot(a, i, t)
+            step = slot(a, i + 1, t) - first
+            if step != S:
+                src = picked[a][:, first : first + rows * step].rearrange("p (i j) -> p i j", i=rows)[:, :, 0:TOK]
+            else:
+                src = picked[a].rearrange("p (i j) -> p i j", i=PACK)[:, i : i + rows, t * TOK : (t + n) * TOK]
+            dst = words_of(units.index((a, t)), n).rearrange("p (c l i) -> p c i l", l=4, i=PACK)
+            nc.scalar.copy(out=dst[:, :, i : i + rows, :], in_=src.rearrange("p i (c l) -> p c i l", l=4))
+
+        def quantise(u, n):
+            cols = slice(u * TOK, (u + n) * TOK)
+            nc.vector.quantize_mx(out=codes[:, cols].bitcast(E4M3X4), scales=scales[:, cols], in_=words_of(u, n))
+            for a, t in sorted(units[u : u + n], key=lambda at: at[1] if at[0] >= 2 else at[0]):
+                multiply(a, t)
 
         def multiply(a, t):
-            cols = slice(a * S + t * TOK, a * S + (t + 1) * TOK)
+            u = units.index((a, t))
+            cols = slice(u * TOK, (u + 1) * TOK)
             nc.tensor.matmul_mx(
                 out=acc[t][:],
                 lhsT=codes[:, cols].bitcast(E4M3X4),
@@ -135,54 +144,43 @@ def tile_list_heads_tm_res_kernel(tc, xT, w_words, w_scales, wgt, r, offs, out):
         nc.sync.dma_start(out=res[1][:, 0, :], in_=r[TOK : 2 * TOK, :])
         nc.sync.dma_start(out=res[2][:], in_=r[2 * TOK : S, :].rearrange("(t p) n -> p t n", p=P))
 
-        for a in range(last):
-            for i in range(PACK):
-                if (a, i) == (0, 0):
-                    gather(a, i, 0, HALF)
-                    gather(a, i, HALF, S)
-                elif i == PACK - 1 and a > 0:
-                    gather(a, i, 0, CUT)
-                    gather(a, i, CUT, S)
-                else:
-                    gather(a, i, 0, S)
-                if (a, i) == (2, 2):
-                    quantise(0, 0, 2 * S)
-                    for b in (0, 1):
-                        for t in range(TOK_TILES):
-                            multiply(b, t)
-            if a == 0:
-                interleave(a, 0, PACK, 0, S)
-            else:
-                interleave(a, 0, PACK, 0, CUT)
-                interleave(a, 0, PACK, CUT, S)
+        gather(0, 0, 0, 2)
+        gather(0, 0, 2, 2)
+        for i in (1, 2, 3):
+            gather(0, i, 0, 4)
+        interleave(0, 0, PACK, 0, 3)
+        for i in range(PACK):
+            gather(1, i, 0, 4)
+        interleave(1, 0, PACK, 0, 4)
+        interleave(0, 0, PACK, 3, 1)
+        for i in range(PACK):
+            gather(2, i, 0, 4)
+            if i == 2:
+                quantise(0, early)
+        interleave(2, 0, PACK, 0, 3)
+        interleave(2, 0, PACK, 3, 1)
 
-        gather(last, 0, 0, S)
-        gather(last, 1, 0, S)
-        interleave(last, 0, 2, 0, TOK)
-        interleave(last, 0, 2, HALF, S)
-        quantise(last - 1, 0, S)
-        for t in range(TOK_TILES):
-            multiply(last - 1, t)
-        gather(last, 2, 0, HALF)
-        gather(last, 3, 0, TOK)
-        interleave(last, 2, 2, 0, TOK)
-        gather(last, 3, TOK, HALF)
-        interleave(last, 0, PACK, TOK, HALF)
-        gather(last, 3, HALF, S)
-        quantise(last, 0, TOK)
-        multiply(last, 0)
+        gather(last, 0, 0, 4)
+        gather(last, 1, 0, 4)
+        interleave(last, 0, 2, 0, 1)
+        interleave(last, 0, 2, 2, 2)
+        quantise(early, 2)
+        gather(last, 2, 0, 2)
+        gather(last, 3, 0, 1)
+        interleave(last, 2, 2, 0, 1)
+        gather(last, 3, 1, 1)
+        interleave(last, 0, PACK, 1, 1)
+        gather(last, 3, 2, 2)
+        quantise(early + 2, 2)
         for t in (2, 3):
-            gather(last, 2, t * TOK, (t + 1) * TOK)
-            interleave(last, 2, 2, t * TOK, (t + 1) * TOK)
-        quantise(last, TOK, 2 * TOK)
-        multiply(last, 1)
+            gather(last, 2, t, 1)
+            interleave(last, 2, 2, t, 1)
+        quantise(early + 4, 2)
         add_residual(0, 0, M)
         store(0)
-        quantise(last, 2 * TOK, 3 * TOK)
-        multiply(last, 2)
+        quantise(early + 6, 1)
         add_residual(1, 0, M // 2)
-        quantise(last, 3 * TOK, S)
-        multiply(last, 3)
+        quantise(early + 7, 1)
         add_residual(1, M // 2, M)
         store(1)
         for t in (2, 3):

@@ -51,7 +51,8 @@ def tile_list_heads_tm_res_kernel(tc, xT, w_words, w_scales, wgt, r, offs, out):
         ww = [keep.tile([P, n, 2 * M], U8, name=f"ww{a}", align_bytes=64) for a, n in word_loads]
         ws = keep.tile([P, PASSES, M], U8, name="ws", align_bytes=64)
         res = [keep.tile([P, n, M], F32, name=f"res{t}") for t, n in ((0, 1), (1, 1), (2, 2))]
-        done = [keep.tile([P, M], F32, name=f"done{t}") for t in range(TOK_TILES)]
+        done = [picked[last][:, 2 * S - TOK : 3 * S - TOK], picked[last][:, 3 * S : 4 * S]]
+        done = done + [keep.tile([P, M], F32, name=f"done{t}")[:] for t in (2, 3)]
         acc = [psum.tile([P, M], F32, name=f"acc{t}") for t in range(TOK_TILES)]
 
         def slot(a, i, t):
@@ -125,7 +126,7 @@ def tile_list_heads_tm_res_kernel(tc, xT, w_words, w_scales, wgt, r, offs, out):
             nc.vector.tensor_tensor(done[t][:, lo:hi], acc[t][:, lo:hi], residual, ADD)
 
         def store(t):
-            nc.sync.dma_start(out=out[t * TOK : (t + 1) * TOK, :], in_=done[t][:])
+            nc.sync.dma_start(out=out[t * TOK : (t + 1) * TOK, :], in_=done[t])
 
         nc.gpsimd.memset(ws[:].rearrange("p a n -> p (a n)").bitcast(I32), 0)
         load_x(0, 0)
@@ -176,13 +177,11 @@ def tile_list_heads_tm_res_kernel(tc, xT, w_words, w_scales, wgt, r, offs, out):
             gather(last, 2, t, 1)
             interleave(last, 2, 2, t, 1)
         quantise(early + 4, 2)
-        add_residual(0, 0, M)
-        store(0)
+        add_residual(0, 0, M // 2)
         quantise(early + 6, 1)
-        add_residual(1, 0, M // 2)
+        add_residual(0, M // 2, M)
+        store(0)
         quantise(early + 7, 1)
-        add_residual(1, M // 2, M)
-        store(1)
-        for t in (2, 3):
+        for t in (1, 2, 3):
             add_residual(t, 0, M)
             store(t)

@@ -39,7 +39,7 @@ def tile_list_heads_tm_res_kernel(tc, xT, w_words, w_scales, wgt, r, offs, out):
         wg = keep.tile([P, S], F32, name="wg")
         picked = [keep.tile([P, PACK * S], F32, name=f"picked{a}", align_bytes=64)[:] for a in (0, 2, 3)]
         units = [(0, 0), (0, 1), (0, 2), (1, 0), (1, 1), (1, 2), (1, 3), (0, 3)]
-        units = units + [(2, 0), (2, 1), (2, 2), (3, 0), (2, 3), (3, 1), (3, 2), (3, 3)]
+        units = units + [(2, 0), (2, 1), (3, 0), (3, 1), (2, 2), (2, 3), (3, 2), (3, 3)]
         early = 2 * TOK_TILES
         unit_words = TOK * PACK // 2
         shared = keep.tile([P, (early - 1) * unit_words + PACK * S], F32, name="shared", align_bytes=64)
@@ -57,7 +57,7 @@ def tile_list_heads_tm_res_kernel(tc, xT, w_words, w_scales, wgt, r, offs, out):
 
         def slot(a, i, t):
             if (a, i, t) == (last, 3, 0):
-                return 2 * S + HALF + TOK // 2
+                return 2 * S + 3 * TOK
             return i * S + t * TOK
 
         def load_x(a, i):
@@ -101,6 +101,14 @@ def tile_list_heads_tm_res_kernel(tc, xT, w_words, w_scales, wgt, r, offs, out):
                 src = picked[a].rearrange("p (i j) -> p i j", i=PACK)[:, i : i + rows, t * TOK : (t + n) * TOK]
             dst = words_of(units.index((a, t)), n).rearrange("p (c l i) -> p c i l", l=4, i=PACK)
             nc.scalar.copy(out=dst[:, :, i : i + rows, :], in_=src.rearrange("p i (c l) -> p c i l", l=4))
+
+        def interleave_halves(a, lo, hi):
+            src = picked[a].rearrange("p (i h j) -> p h i j", i=PACK, h=2)[:, :, :, lo:hi]
+            dst = words_of(units.index((a, 0)), 8).rearrange("p (h j i) -> p h j i", h=2, i=PACK)[:, :, lo:hi, :]
+            nc.scalar.copy(
+                out=dst.rearrange("p h (c l) i -> p h c i l", l=4),
+                in_=src.rearrange("p h i (c l) -> p h c i l", l=4),
+            )
 
         def quantise(u, n):
             cols = slice(u * TOK, (u + n) * TOK)
@@ -158,28 +166,27 @@ def tile_list_heads_tm_res_kernel(tc, xT, w_words, w_scales, wgt, r, offs, out):
             gather(2, i, 0, 4)
             if i == 2:
                 quantise(0, early)
-        interleave(2, 0, PACK, 0, 3)
-        interleave(2, 0, PACK, 3, 1)
+        interleave_halves(2, 0, 192)
+        interleave_halves(2, 192, HALF)
 
         gather(last, 0, 0, 4)
         gather(last, 1, 0, 4)
         interleave(last, 0, 2, 0, 1)
         interleave(last, 0, 2, 2, 2)
-        quantise(early, 2)
-        gather(last, 2, 0, 2)
+        quantise(early, 1)
+        gather(last, 2, 0, 3)
         gather(last, 3, 0, 1)
         interleave(last, 2, 2, 0, 1)
         gather(last, 3, 1, 1)
         interleave(last, 0, PACK, 1, 1)
         gather(last, 3, 2, 2)
-        quantise(early + 2, 2)
-        for t in (2, 3):
-            gather(last, 2, t, 1)
-            interleave(last, 2, 2, t, 1)
-        quantise(early + 4, 2)
-        add_residual(0, 0, M // 2)
-        quantise(early + 6, 1)
-        add_residual(0, M // 2, M)
+        interleave(last, 2, 2, 2, 1)
+        quantise(early + 1, 2)
+        gather(last, 2, 3, 1)
+        interleave(last, 2, 2, 3, 1)
+        quantise(early + 3, 2)
+        quantise(early + 5, 2)
+        add_residual(0, 0, M)
         store(0)
         quantise(early + 7, 1)
         for t in (1, 2, 3):

@@ -35,7 +35,7 @@ def tile_list_heads_tm_res_kernel(tc, xT, w_words, w_scales, wgt, r, offs, out):
 
         last = PASSES - 1
         offsets = lists.tile([P, S // PER_COL], U16, name="offsets")
-        x = [[keep.tile([P, T], F32, name=f"x{a}_{i}", align_bytes=64) for i in range(PACK)] for a in range(PASSES)]
+        x = [[keep.tile([P, T], F32, name=f"x{a}_{i}", tag=f"x{a}_{i}", align_bytes=64) for i in range(PACK)] for a in range(PASSES)]
         wg = keep.tile([P, S], F32, name="wg")
         picked = [keep.tile([P, PACK * S], F32, name=f"picked{a}", align_bytes=64)[:] for a in (0, 2, 3)]
         units = [(0, 0), (0, 1), (0, 2), (1, 0), (1, 1), (1, 2), (1, 3), (0, 3)]
@@ -54,6 +54,8 @@ def tile_list_heads_tm_res_kernel(tc, xT, w_words, w_scales, wgt, r, offs, out):
         done = [picked[last][:, 2 * S - TOK : 3 * S - TOK], picked[last][:, 3 * S : 4 * S]]
         done = done + [keep.tile([P, M], F32, name=f"done{t}")[:] for t in (2, 3)]
         acc = [psum.tile([P, M], F32, name=f"acc{t}") for t in range(TOK_TILES)]
+
+        held = {}
 
         def slot(a, i, t):
             if (a, i, t) == (last, 3, 0):
@@ -110,9 +112,14 @@ def tile_list_heads_tm_res_kernel(tc, xT, w_words, w_scales, wgt, r, offs, out):
                 in_=src.rearrange("p h i (c l) -> p h c i l", l=4),
             )
 
+        def codes_of(u, n):
+            if u in held:
+                return held[u][:].bitcast(E4M3X4)
+            return codes[:, u * TOK : (u + n) * TOK].bitcast(E4M3X4)
+
         def quantise(u, n):
             cols = slice(u * TOK, (u + n) * TOK)
-            nc.vector.quantize_mx(out=codes[:, cols].bitcast(E4M3X4), scales=scales[:, cols], in_=words_of(u, n))
+            nc.vector.quantize_mx(out=codes_of(u, n), scales=scales[:, cols], in_=words_of(u, n))
             for a, t in sorted(units[u : u + n], key=lambda at: at[1] if at[0] >= 2 else at[0]):
                 multiply(a, t)
 
@@ -121,7 +128,7 @@ def tile_list_heads_tm_res_kernel(tc, xT, w_words, w_scales, wgt, r, offs, out):
             cols = slice(u * TOK, (u + 1) * TOK)
             nc.tensor.matmul_mx(
                 out=acc[t][:],
-                lhsT=codes[:, cols].bitcast(E4M3X4),
+                lhsT=codes_of(u, 1),
                 lhsT_scale=scales[:, cols],
                 rhs=ww[a // last][:, a % last, :].bitcast(E2M1X4),
                 rhs_scale=ws[:, a, :],
@@ -185,7 +192,9 @@ def tile_list_heads_tm_res_kernel(tc, xT, w_words, w_scales, wgt, r, offs, out):
         gather(last, 2, 3, 1)
         interleave(last, 2, 2, 3, 1)
         quantise(early + 3, 2)
-        quantise(early + 5, 2)
+        held[early + 5] = keep.tile([P, TOK], U32, name="late_codes", tag="x3_2", align_bytes=64)
+        quantise(early + 5, 1)
+        quantise(early + 6, 1)
         add_residual(0, 0, M)
         store(0)
         quantise(early + 7, 1)

from contextlib import ExitStack

import concourse.mybir as mybir

K, M, T, S = 2048, 512, 1024, 512
FLOPS = 2 * K * M * S

F32 = mybir.dt.float32
BF16 = mybir.dt.bfloat16
I32 = mybir.dt.int32
U32 = mybir.dt.uint32
U16 = mybir.dt.uint16
U8 = mybir.dt.uint8
E4M3X4 = mybir.dt.float8_e4m3fn_x4
E2M1X4 = mybir.dt.float4_e2m1fn_x4
MULT = mybir.AluOpType.mult
ADD = mybir.AluOpType.add

P = 128
PACK = 4
K_PASS = P * PACK
PASSES = K // K_PASS
TOK = 128
TOK_TILES = S // TOK
HALF = S // 2
PER_COL = 16


def tile_list_heads_tm_res_kernel(tc, xT, w_words, w_scales, wgt, r, offs, out):
    nc = tc.nc
    with ExitStack() as ctx:
        lists = ctx.enter_context(tc.tile_pool(name="lists", bufs=1))
        keep = ctx.enter_context(tc.tile_pool(name="keep", bufs=1))
        psum = ctx.enter_context(tc.psum_pool(name="psum", bufs=1))

        last = PASSES - 1
        offsets = lists.tile([P, S // PER_COL], U16, name="offsets")
        x = [[keep.tile([P, T], F32, name=f"x{a}_{i}", tag=f"x{a}_{i}", align_bytes=64) for i in range(PACK)] for a in range(PASSES)]
        wg = keep.tile([P, S], F32, name="wg")
        picked = [keep.tile([P, PACK * S], F32, name=f"picked{a}", align_bytes=64)[:] for a in (0, 2, 3)]
        units = [(0, 0), (0, 1), (0, 2), (1, 0), (1, 1), (1, 2), (1, 3), (0, 3)]
        units = units + [(2, 0), (2, 1), (3, 0), (3, 1), (2, 2), (2, 3), (3, 2), (3, 3)]
        early = 2 * TOK_TILES
        unit_words = TOK * PACK // 2
        shared = keep.tile([P, (early - 1) * unit_words + PACK * S], F32, name="shared", align_bytes=64)
        picked.insert(1, shared[:, (early - 1) * unit_words :])
        late = keep.tile([P, (len(units) - early) * TOK * PACK], BF16, name="late", align_bytes=64)
        codes = keep.tile([P, PASSES * S], U32, name="codes", align_bytes=64)
        scales = keep.tile([P, PASSES * S], U8, name="scales", align_bytes=64)
        word_loads = ((0, 3), (3, 1))
        ww = [keep.tile([P, n, 2 * M], U8, name=f"ww{a}", align_bytes=64) for a, n in word_loads]
        ws = keep.tile([P, PASSES, M], U8, name="ws", align_bytes=64)
        res = [keep.tile([P, n, M], F32, name=f"res{t}") for t, n in ((0, 1), (1, 1), (2, 2))]
        done = [picked[last][:, 2 * S - TOK : 3 * S - TOK], picked[last][:, 3 * S : 4 * S]]
        done = done + [keep.tile([P, M], F32, name=f"done{t}")[:] for t in (2, 3)]
        acc = [psum.tile([P, M], F32, name=f"acc{t}") for t in range(TOK_TILES)]

        held = {}

        def slot(a, i, t):
            if (a, i, t) == (last, 3, 0):
                return 2 * S + 3 * TOK
            return i * S + t * TOK

        def load_x(a, i):
            rows = xT[a * K_PASS : (a + 1) * K_PASS, :].rearrange("(p i) t -> p i t", i=PACK)
            nc.sync.dma_start(out=x[a][i][:], in_=rows[:, i, :])

        def load_scales():
            for u in range(4):
                nc.sync.dma_start(
                    out=ws[u:P:32, :, :].bitcast(I32),
                    in_=w_scales[:, u:16:4, :].rearrange("a q n -> q a n").bitcast(I32),
                )

        def load_words(h):
            first, n = word_loads[h]
            nc.sync.dma_start(
                out=ww[h][:].bitcast(I32),
                in_=w_words[first : first + n].rearrange("a p n -> p a n").bitcast(I32),
            )

        def gather(a, i, t, n):
            at = slot(a, i, t)
            nc.vector.tensor_tensor(
                picked[a][:, at : at + n * TOK],
                x[a][i][:].indirect(offsets[:, t * TOK // PER_COL : (t + n) * TOK // PER_COL]),
                wg[:, t * TOK : (t + n) * TOK],
                MULT,
            )

        def words_of(u, n):
            if u < early:
                return shared[:, u * unit_words : (u + n) * unit_words].bitcast(BF16)
            return late[:, (u - early) * TOK * PACK : (u - early + n) * TOK * PACK]

        def interleave(a, i, rows, t, n):
            first = slot(a, i, t)
            step = slot(a, i + 1, t) - first
            if step != S:
                src = picked[a][:, first : first + rows * step].rearrange("p (i j) -> p i j", i=rows)[:, :, 0:TOK]
            else:
                src = picked[a].rearrange("p (i j) -> p i j", i=PACK)[:, i : i + rows, t * TOK : (t + n) * TOK]
            dst = words_of(units.index((a, t)), n).rearrange("p (c l i) -> p c i l", l=4, i=PACK)
            nc.scalar.copy(out=dst[:, :, i : i + rows, :], in_=src.rearrange("p i (c l) -> p c i l", l=4))

        def interleave_halves(a, lo, hi):
            src = picked[a].rearrange("p (i h j) -> p h i j", i=PACK, h=2)[:, :, :, lo:hi]
            dst = words_of(units.index((a, 0)), 8).rearrange("p (h j i) -> p h j i", h=2, i=PACK)[:, :, lo:hi, :]
            nc.scalar.copy(
                out=dst.rearrange("p h (c l) i -> p h c i l", l=4),
                in_=src.rearrange("p h i (c l) -> p h c i l", l=4),
            )

        def codes_of(u, n):
            if u in held:
                return held[u][:].bitcast(E4M3X4)
            return codes[:, u * TOK : (u + n) * TOK].bitcast(E4M3X4)

        def quantise(u, n):
            cols = slice(u * TOK, (u + n) * TOK)
            nc.vector.quantize_mx(out=codes_of(u, n), scales=scales[:, cols], in_=words_of(u, n))
            for a, t in sorted(units[u : u + n], key=lambda at: at[1] if at[0] >= 2 else at[0]):
                multiply(a, t)

        def multiply(a, t):
            u = units.index((a, t))
            cols = slice(u * TOK, (u + 1) * TOK)
            nc.tensor.matmul_mx(
                out=acc[t][:],
                lhsT=codes_of(u, 1),
                lhsT_scale=scales[:, cols],
                rhs=ww[a // last][:, a % last, :].bitcast(E2M1X4),
                rhs_scale=ws[:, a, :],
                start=(a == 0),
                stop=(a == last),
            )

        def add_residual(t, lo, hi):
            residual = res[min(t, 2)][:, max(t - 2, 0), lo:hi]
            nc.vector.tensor_tensor(done[t][:, lo:hi], acc[t][:, lo:hi], residual, ADD)

        def store(t):
            nc.sync.dma_start(out=out[t * TOK : (t + 1) * TOK, :], in_=done[t])

        nc.gpsimd.memset(ws[:].rearrange("p a n -> p (a n)").bitcast(I32), 0)
        load_x(0, 0)
        nc.scalar.dma_start(out=wg[:, 0:HALF], in_=wgt[:, 0:HALF])
        nc.sync.dma_start(offsets[:], offs)
        nc.sync.dma_start(out=wg[:, HALF:S], in_=wgt[:, HALF:S])
        for a in range(PASSES):
            for i in range(PACK):
                if (a, i) == (last, 2):
                    load_scales()
                    load_words(0)
                if (a, i) != (0, 0):
                    load_x(a, i)
        load_words(1)
        nc.sync.dma_start(out=res[0][:, 0, :], in_=r[0:TOK, :])
        nc.sync.dma_start(out=res[1][:, 0, :], in_=r[TOK : 2 * TOK, :])
        nc.sync.dma_start(out=res[2][:], in_=r[2 * TOK : S, :].rearrange("(t p) n -> p t n", p=P))

        gather(0, 0, 0, 2)
        gather(0, 0, 2, 2)
        for i in (1, 2, 3):
            gather(0, i, 0, 4)
        interleave(0, 0, PACK, 0, 3)
        for i in range(PACK):
            gather(1, i, 0, 4)
        interleave(1, 0, PACK, 0, 4)
        interleave(0, 0, PACK, 3, 1)
        for i in range(PACK):
            gather(2, i, 0, 4)
            if i == 2:
                quantise(0, early)
        interleave_halves(2, 0, 192)
        interleave_halves(2, 192, HALF)

        gather(last, 0, 0, 4)
        gather(last, 1, 0, 4)
        interleave(last, 0, 2, 0, 1)
        interleave(last, 0, 2, 2, 2)
        quantise(early, 1)
        gather(last, 2, 0, 3)
        gather(last, 3, 0, 1)
        interleave(last, 2, 2, 0, 1)
        gather(last, 3, 1, 1)
        interleave(last, 0, PACK, 1, 1)
        gather(last, 3, 2, 2)
        interleave(last, 2, 2, 2, 1)
        quantise(early + 1, 2)
        gather(last, 2, 3, 1)
        interleave(last, 2, 2, 3, 1)
        quantise(early + 3, 2)
        held[early + 5] = keep.tile([P, TOK], U32, name="late_codes", tag="x3_2", align_bytes=64)
        quantise(early + 5, 1)
        quantise(early + 6, 1)
        add_residual(0, 0, M)
        store(0)
        quantise(early + 7, 1)
        for t in (1, 2, 3):
            add_residual(t, 0, M)
            store(t)
